import numpy as np
import ml_dtypes


def mxq(x, axis, fmt="e4m3"):
    dtype, down = {"e4m3": (ml_dtypes.float8_e4m3fn, 7), "e5m2": (ml_dtypes.float8_e5m2, 14)}[fmt]
    v = np.moveaxis(np.asarray(x, np.float32).astype(ml_dtypes.bfloat16).astype(np.float64), axis, -1)
    blocks = v.reshape(v.shape[:-1] + (-1, 32))
    amax = np.abs(blocks).max(-1, keepdims=True)
    byte = np.maximum(np.where(amax > 0, np.frexp(amax)[1] - 1 + 127, 0) - down, 1)
    scale = np.exp2(byte - 127.0)
    codes = (blocks / scale).astype(np.float32).astype(dtype).astype(np.float64)
    return np.moveaxis((codes * scale).reshape(v.shape), -1, axis)


WIDE = False


def mx_kscale(k):
    if not WIDE:
        return np.ones(k)
    levels = np.array([10, -10, 5, -5, 0])
    if k % 512:
        return np.exp2(np.random.permutation(np.resize(levels, k // 32))).repeat(32)
    a = np.empty((k // 512, 16))
    for p in range(k // 512):
        a[p, :8] = np.random.permutation(np.resize(levels, 8))
        for g in range(8):
            far = levels[np.abs(levels - a[p, g]) >= 10]
            a[p, g + 8] = far[np.random.randint(len(far))]
    return np.exp2(a.ravel()).repeat(32)


def f64(x):
    return np.asarray(x).astype(np.float64)


def striped(idx):
    return np.tile(idx.reshape(-1, 16).T, (8, 1)).astype(np.uint16)


def unstriped(offs):
    return offs[:16].T.reshape(-1).astype(np.int64)


E2M1 = np.array([0.0, 0.5, 1.0, 1.5, 2.0, 3.0, 4.0, 6.0, -0.0, -0.5, -1.0, -1.5, -2.0, -3.0, -4.0, -6.0])


def pack_weight(w, fmt):
    k, n = w.shape
    w = f64(np.asarray(w, np.float32).astype(ml_dtypes.bfloat16)).reshape(k // 32, 32, n)
    amax = np.abs(w).max(1)
    if fmt == "e4m3":
        byte = np.frexp(amax)[1] - 1 + 127 - 7
    else:
        mant, ex = np.frexp(amax / 6.0)
        byte = np.where(mant > 0.5, ex, ex - 1) + 127
    byte = np.clip(np.where(amax > 0, byte, 1), 1, 254)
    scaled = (w * np.exp2(127.0 - byte)[:, None, :]).reshape(k, n).astype(np.float32)
    by_word = np.ascontiguousarray(scaled.reshape(k // 512, 128, 4, n).transpose(0, 1, 3, 2))
    if fmt == "e4m3":
        words = by_word.astype(ml_dtypes.float8_e4m3fn).view(np.uint8)
    else:
        c = by_word.astype(ml_dtypes.float4_e2m1fn).view(np.uint8) & 0xF
        words = (c[..., 0::2] | (c[..., 1::2] << 4)).reshape(k // 512, 128, 2 * n)
    return np.ascontiguousarray(words), np.ascontiguousarray(byte.astype(np.uint8).reshape(k // 512, 16, n))


def unpack_weight(words, scales, fmt):
    g, _, n = scales.shape
    words = np.ascontiguousarray(words).reshape(g, 128, n, -1)
    if fmt == "e4m3":
        vals = words.view(ml_dtypes.float8_e4m3fn).astype(np.float64)
    else:
        nib = np.empty((g, 128, n, 4), np.uint8)
        nib[..., 0::2] = words & 0xF
        nib[..., 1::2] = words >> 4
        vals = E2M1[nib]
    vals = vals * np.repeat(np.exp2(scales.astype(np.float64) - 127.0), 8, axis=1)[..., None]
    return vals.transpose(0, 1, 3, 2).reshape(g * 512, n)


def gelu(v):
    return 0.5 * v * (1.0 + np.tanh(np.sqrt(2.0 / np.pi) * (v + 0.044715 * v**3)))


K, T, S, S2 = 1024, 2048, 512, 1024

def setup_inputs():
    n = np.random.standard_normal
    s = mx_kscale(K)[:, None]
    d = {}
    d["tab_words"], d["tab_scales"] = pack_weight(n((K, T)) * s, "e4m3")
    d["offs"] = striped(np.random.permutation(T)[:S])
    d["offs2"] = striped(np.random.permutation(T)[:S2])
    d["w1"] = (n((K, K)) / K / s / s.T).astype(np.float32)
    d["w2_words"], d["w2_scales"] = pack_weight(n((K, K)) / K / s / s.T, "e2m1")
    d["obs"] = (0.9 * n((S2, S))).astype(np.float32)
    return d

def reference(tab_words, tab_scales, offs, offs2, w1, w2_words, w2_scales, obs):
    TW = unpack_weight(tab_words, tab_scales, "e4m3")
    v = TW[:, unstriped(offs)]
    v2 = TW[:, unstriped(offs2)]
    w2 = unpack_weight(w2_words, w2_scales, "e2m1")
    space = mxq(f64(w1), 0, "e4m3").T @ v
    food = w2.T @ v
    h = np.maximum(space, food)
    e = v2.T @ mxq(h, 0, "e4m3")
    diff = e - f64(obs)
    return np.square(diff)

from contextlib import ExitStack

import concourse.mybir as mybir

K, T, S, S2 = 1024, 2048, 512, 1024
FLOPS = 2 * (2 * K * K * S + K * S2 * S)

F32 = mybir.dt.float32
BF16 = mybir.dt.bfloat16
I32 = mybir.dt.int32
U32 = mybir.dt.uint32
U16 = mybir.dt.uint16
U8 = mybir.dt.uint8
FP8X4 = mybir.dt.float8_e4m3fn_x4
FP4X4 = mybir.dt.float4_e2m1fn_x4
ALU = mybir.AluOpType
ACT = mybir.ActivationFunctionType

P = 128
PACK = 4
K_PASS = P * PACK
PASSES = K // K_PASS
QUADS = 4
J_TILE = 128
J_HALF = 256


def tile_list_cohabitation_tension_scores_kernel(
    tc, tab_words, tab_scales, offs, offs2, w1, w2_words, w2_scales, obs, out
):
    nc = tc.nc
    with ExitStack() as ctx:
        held = ctx.enter_context(tc.tile_pool(name="held", bufs=1))
        ring = ctx.enter_context(tc.tile_pool(name="ring", bufs=3))
        psum = ctx.enter_context(tc.psum_pool(name="psum", bufs=8))

        def keep(name, shape, dtype, tag=""):
            return held.tile(shape, dtype, name=name, tag=tag or name, align_bytes=64)

        arrivals = held.tile([P, S // 16], U16, name="arrivals")
        residents = held.tile([P, S2 // 16], U16, name="residents")
        tab_sc = keep("tab_sc", [P, T], U8)
        w2_sc_raw = keep("w2_sc_raw", [P, K], U8)
        both_sc = keep("both_sc", [P, K + S], U8)
        pass1_sc = keep("pass1_sc", [P, K + S], U8)
        warm = keep("warm", [P, 8], F32)
        warm_out = keep("warm_out", [P, 8], F32)

        nc.vector.memset(tab_sc[:].bitcast(I32), 0)
        nc.vector.memset(w2_sc_raw[:].bitcast(I32), 0)
        nc.vector.memset(pass1_sc[:].bitcast(I32), 0)
        nc.vector.memset(warm[:], 0.0)
        nc.scalar.activation(out=warm_out[:], in_=warm[:], func=ACT.Square)

        nc.sync.dma_start(arrivals[:], offs)
        for q in range(QUADS):
            nc.sync.dma_start(
                out=tab_sc[32 * q : 32 * q + 8, :].bitcast(I32),
                in_=tab_scales[:, 4 * q : 4 * q + 4, :].bitcast(I32),
            )
        w1_raw = {}

        def load_w1(a, b, tag):
            w1_raw[a, b] = keep(f"w1_raw{a}{b}", [P, PACK, K_PASS], F32, tag)
            rows = w1[a * K_PASS : (a + 1) * K_PASS, b * K_PASS : (b + 1) * K_PASS]
            nc.sync.dma_start(out=w1_raw[a, b][:], in_=rows.rearrange("(p i) c -> p i c", i=PACK))

        tab_w = {}

        def load_tab(a, tag=""):
            tab_w[a] = keep(f"tab_w{a}", [P, T], I32, tag)
            nc.sync.dma_start(out=tab_w[a][:], in_=tab_words[a].rearrange("p t i -> p (t i)").bitcast(I32))

        obs_sb = {}

        def load_obs(s, tag):
            obs_sb[s] = keep(f"obs{s}", [P, 4, S], F32, tag)
            nc.sync.dma_start(
                out=obs_sb[s][:], in_=obs[s * 512 : (s + 1) * 512, :].rearrange("(u p) j -> p u j", p=P)
            )

        nc.sync.dma_start(residents[:], offs2)
        load_w1(0, 0, "stage_x")
        w2_raw = keep("w2_raw", [P, PASSES, K // 2], I32, "stage_y")
        nc.sync.dma_start(out=w2_raw[:], in_=w2_words.bitcast(I32).rearrange("a p c -> p a c"))
        for q in range(QUADS):
            nc.sync.dma_start(
                out=w2_sc_raw[32 * q : 32 * q + 8, :].bitcast(I32),
                in_=w2_scales[:, 4 * q : 4 * q + 4, :].bitcast(I32),
            )

        load_tab(0, "stage_w")
        load_w1(1, 0, "stage_z")
        load_tab(1)

        w1_bf, w1_q, w1_sc = {}, {}, {}

        def cast_w1(a, b, vector_share=0):
            w1_bf[a, b] = keep(f"w1_bf{a}{b}", [P, PACK * K_PASS], BF16)
            dealt = w1_bf[a, b][:].rearrange("p (t m i) -> p m i t", t=PACK, i=PACK)
            raw = w1_raw[a, b][:].rearrange("p i (m t) -> p m i t", t=PACK)
            nc.scalar.copy(out=dealt[:, vector_share:], in_=raw[:, vector_share:])
            if vector_share:
                nc.vector.tensor_copy(out=dealt[:, :vector_share], in_=raw[:, :vector_share])

        def quantize_w1(a, b):
            w1_q[a, b] = keep(f"w1_q{a}{b}", [P, K_PASS], U32)
            w1_sc[a, b] = keep(f"w1_sc{a}{b}", [P, K_PASS], U8)
            nc.vector.quantize_mx(out=w1_q[a, b][:].bitcast(FP8X4), scales=w1_sc[a, b][:], in_=w1_bf[a, b][:])

        def gather_words(name, a, offsets, count=S):
            picked = keep(name, [P, count], U32)
            nc.vector.tensor_copy(picked[:], tab_w[a][:].bitcast(U32).indirect(offsets))
            return picked

        def gather_scales(name, offsets, count=S):
            picked = keep(name, [P, count], U8)
            nc.vector.tensor_copy(picked[:], tab_sc[:].indirect(offsets))
            return picked

        v_sc = gather_scales("v_sc", arrivals[:])
        nc.vector.tensor_copy(out=both_sc[:, K : K + S].bitcast(I32), in_=v_sc[:].bitcast(I32))
        r_sc = gather_scales("r_sc", residents[:], S2)
        cast_w1(0, 0)
        nc.vector.tensor_copy(
            out=both_sc[:, 0:K].rearrange("p (b t g m) -> p b g t m", b=PASSES, t=PACK, m=16),
            in_=w2_sc_raw[:].rearrange("p (b g m t) -> p b g t m", b=PASSES, t=PACK, m=16),
        )
        for q in range(QUADS):
            nc.sync.dma_start(
                out=pass1_sc[32 * q : 32 * q + 4, :].bitcast(I32),
                in_=both_sc[32 * q + 4 : 32 * q + 8, :].bitcast(I32),
            )
        load_w1(0, 1, "stage_x")
        w2_q = keep("w2_q", [P, PASSES * K * 2], U8)
        nc.vector.tensor_copy(
            out=w2_q[:].bitcast(U16).rearrange("p (c t g m) -> p c g t m", t=PACK, g=16, m=8),
            in_=w2_raw[:].rearrange("p a c -> p (a c)").bitcast(U16).rearrange("p (c g m t) -> p c g t m", t=PACK, g=16, m=8),
        )
        load_w1(1, 1, "stage_y")
        quantize_w1(0, 0)
        v_w = {0: gather_words("v_w0", 0, arrivals[:])}
        r_w = {0: gather_words("r_w0", 0, residents[:], S2)}
        cast_w1(1, 0)
        load_obs(0, "stage_z")
        load_obs(1, "stage_w")
        v_w[1] = gather_words("v_w1", 1, arrivals[:])
        quantize_w1(1, 0)

        food_sb, h_bf, h_q, h_sc = {}, {}, {}, {}

        def food(b, c, place):
            bank = psum.tile([P, PACK, J_TILE], F32, name="food_bank", tag="bank")
            cols = slice(c * J_TILE, (c + 1) * J_TILE)
            for t in range(PACK):
                for a in range(PASSES):
                    col = b * K_PASS + t * P
                    planes = (both_sc, pass1_sc)[a]
                    nc.tensor.matmul_mx(
                        out=bank[:, t, :],
                        lhsT=w2_q[:, 2 * (a * K + col) : 2 * (a * K + col + P)].bitcast(FP4X4),
                        lhsT_scale=planes[:, col : col + P],
                        rhs=v_w[a][:, cols].bitcast(FP8X4),
                        rhs_scale=planes[:, K + c * J_TILE : K + (c + 1) * J_TILE],
                        start=(a == 0),
                        stop=(a == PASSES - 1),
                    )
            food_sb[b, c] = place.rearrange("p (n t) -> p n t", t=PACK)
            nc.scalar.copy(out=food_sb[b, c], in_=bank[:].rearrange("p t n -> p n t"))

        def space_and_max(b, c):
            bank = psum.tile([P, PACK, J_TILE], F32, name="space_bank", tag="bank")
            cols = slice(c * J_TILE, (c + 1) * J_TILE)
            for t in range(PACK):
                for a in range(PASSES):
                    nc.tensor.matmul_mx(
                        out=bank[:, t, :],
                        lhsT=w1_q[a, b][:, t * P : (t + 1) * P].bitcast(FP8X4),
                        lhsT_scale=w1_sc[a, b][:, t * P : (t + 1) * P],
                        rhs=v_w[a][:, cols].bitcast(FP8X4),
                        rhs_scale=v_sc[4 * a :, cols],
                        start=(a == 0),
                        stop=(a == PASSES - 1),
                    )
            half, part = divmod(c, 2)
            if part == 0:
                h_bf[b, half] = keep(f"h_bf{b}{half}", [P, J_HALF * PACK], BF16)
            width = J_TILE * PACK
            nc.vector.tensor_tensor(
                out=h_bf[b, half][:, part * width : (part + 1) * width].rearrange("p (n t) -> p n t", t=PACK),
                in0=bank[:].rearrange("p t n -> p n t"),
                in1=food_sb[b, c],
                op=ALU.max,
            )

        def quantize_h(b, half):
            h_q[b, half] = keep(f"h_q{b}{half}", [P, J_HALF], U32)
            h_sc[b, half] = keep(f"h_sc{b}{half}", [P, J_HALF], U8)
            nc.vector.quantize_mx(out=h_q[b, half][:].bitcast(FP8X4), scales=h_sc[b, half][:], in_=h_bf[b, half][:])

        def score(half, u):
            s, first = divmod(2 * u, 4)
            bank = psum.tile([P, 2, J_HALF], F32, name="e_bank", tag="bank")
            for b in range(PASSES):
                for x in range(2):
                    cols = slice((2 * u + x) * P, (2 * u + x + 1) * P)
                    nc.tensor.matmul_mx(
                        out=bank[:, x, :],
                        lhsT=r_w[b][:, cols].bitcast(FP8X4),
                        lhsT_scale=r_sc[4 * b :, cols],
                        rhs=h_q[b, half][:].bitcast(FP8X4),
                        rhs_scale=h_sc[b, half][:],
                        start=(b == 0 and x == 0),
                        stop=(b == PASSES - 1 and x == 1),
                    )
            js = slice(half * J_HALF, (half + 1) * J_HALF)
            diff = ring.tile([P, 2, J_HALF], F32, name="diff")
            nc.vector.tensor_tensor(out=diff[:], in0=bank[:], in1=obs_sb[s][:, first : first + 2, js], op=ALU.subtract)
            result = keep(f"result{half}{u}", [P, 2, J_HALF], F32)
            nc.scalar.activation(out=result[:], in_=diff[:], func=ACT.Square)
            rows = out[2 * u * P : (2 * u + 2) * P, js]
            nc.sync.dma_start(out=rows.rearrange("(x p) j -> p x j", p=P), in_=result[:])

        cast_w1(0, 1)
        early = keep("food_early", [P, 2, 512], F32, "stage_x")
        food(0, 0, early[:, 0, :])
        food(0, 1, early[:, 1, :])
        r_w[1] = gather_words("r_w1", 1, residents[:], S2)
        quantize_w1(0, 1)
        cast_w1(1, 1, vector_share=32)
        late = keep("food_late", [P, 6, 512], F32, "stage_y")
        space_and_max(0, 0)
        space_and_max(0, 1)
        food(0, 2, late[:, 0, :])
        food(0, 3, late[:, 1, :])
        quantize_w1(1, 1)
        quantize_h(0, 0)
        space_and_max(0, 2)
        food(1, 0, late[:, 2, :])
        space_and_max(0, 3)
        food(1, 1, late[:, 3, :])
        space_and_max(1, 0)
        quantize_h(0, 1)
        space_and_max(1, 1)
        food(1, 2, late[:, 4, :])
        food(1, 3, late[:, 5, :])
        space_and_max(1, 2)
        quantize_h(1, 0)
        space_and_max(1, 3)
        score(0, 0)
        quantize_h(1, 1)
        for u in range(1, 4):
            score(0, u)
        for u in range(4):
            score(1, u)
